import numpy as np
import ml_dtypes


def mxq(x, axis, fmt="e4m3"):
    dtype, down = {"e4m3": (ml_dtypes.float8_e4m3fn, 7), "e5m2": (ml_dtypes.float8_e5m2, 14)}[fmt]
    v = np.moveaxis(np.asarray(x, np.float32).astype(ml_dtypes.bfloat16).astype(np.float64), axis, -1)
    blocks = v.reshape(v.shape[:-1] + (-1, 32))
    amax = np.abs(blocks).max(-1, keepdims=True)
    byte = np.maximum(np.where(amax > 0, np.frexp(amax)[1] - 1 + 127, 0) - down, 1)
    scale = np.exp2(byte - 127.0)
    codes = (blocks / scale).astype(np.float32).astype(dtype).astype(np.float64)
    return np.moveaxis((codes * scale).reshape(v.shape), -1, axis)


WIDE = False


def mx_kscale(k):
    if not WIDE:
        return np.ones(k)
    levels = np.array([10, -10, 5, -5, 0])
    if k % 512:
        return np.exp2(np.random.permutation(np.resize(levels, k // 32))).repeat(32)
    a = np.empty((k // 512, 16))
    for p in range(k // 512):
        a[p, :8] = np.random.permutation(np.resize(levels, 8))
        for g in range(8):
            far = levels[np.abs(levels - a[p, g]) >= 10]
            a[p, g + 8] = far[np.random.randint(len(far))]
    return np.exp2(a.ravel()).repeat(32)


def f64(x):
    return np.asarray(x).astype(np.float64)


def striped(idx):
    return np.tile(idx.reshape(-1, 16).T, (8, 1)).astype(np.uint16)


def unstriped(offs):
    return offs[:16].T.reshape(-1).astype(np.int64)


E2M1 = np.array([0.0, 0.5, 1.0, 1.5, 2.0, 3.0, 4.0, 6.0, -0.0, -0.5, -1.0, -1.5, -2.0, -3.0, -4.0, -6.0])


def pack_weight(w, fmt):
    k, n = w.shape
    w = f64(np.asarray(w, np.float32).astype(ml_dtypes.bfloat16)).reshape(k // 32, 32, n)
    amax = np.abs(w).max(1)
    if fmt == "e4m3":
        byte = np.frexp(amax)[1] - 1 + 127 - 7
    else:
        mant, ex = np.frexp(amax / 6.0)
        byte = np.where(mant > 0.5, ex, ex - 1) + 127
    byte = np.clip(np.where(amax > 0, byte, 1), 1, 254)
    scaled = (w * np.exp2(127.0 - byte)[:, None, :]).reshape(k, n).astype(np.float32)
    by_word = np.ascontiguousarray(scaled.reshape(k // 512, 128, 4, n).transpose(0, 1, 3, 2))
    if fmt == "e4m3":
        words = by_word.astype(ml_dtypes.float8_e4m3fn).view(np.uint8)
    else:
        c = by_word.astype(ml_dtypes.float4_e2m1fn).view(np.uint8) & 0xF
        words = (c[..., 0::2] | (c[..., 1::2] << 4)).reshape(k // 512, 128, 2 * n)
    return np.ascontiguousarray(words), np.ascontiguousarray(byte.astype(np.uint8).reshape(k // 512, 16, n))


def unpack_weight(words, scales, fmt):
    g, _, n = scales.shape
    words = np.ascontiguousarray(words).reshape(g, 128, n, -1)
    if fmt == "e4m3":
        vals = words.view(ml_dtypes.float8_e4m3fn).astype(np.float64)
    else:
        nib = np.empty((g, 128, n, 4), np.uint8)
        nib[..., 0::2] = words & 0xF
        nib[..., 1::2] = words >> 4
        vals = E2M1[nib]
    vals = vals * np.repeat(np.exp2(scales.astype(np.float64) - 127.0), 8, axis=1)[..., None]
    return vals.transpose(0, 1, 3, 2).reshape(g * 512, n)


def gelu(v):
    return 0.5 * v * (1.0 + np.tanh(np.sqrt(2.0 / np.pi) * (v + 0.044715 * v**3)))


K, T, S, P, H, N = 1024, 2048, 1024, 512, 1024, 384


def setup_inputs():
    n = np.random.standard_normal
    s = mx_kscale(K)[:, None]
    u = mx_kscale(H)[:, None]
    tab_words, tab_scales = pack_weight(n((K, T)) * s, "e4m3")
    w2_words, w2_scales = pack_weight(n((K, H)) / np.sqrt(K) / s, "e2m1")
    return {
        "tab_words": tab_words, "tab_scales": tab_scales,
        "offs": striped(np.random.permutation(T)[:S]),
        "pos1": striped(np.random.permutation(S)[:P]),
        "pos2": striped(np.random.permutation(S)[:P]),
        "w1": (0.6 * n((K, H)) / np.sqrt(K) / s).astype(np.float32),
        "focus": (0.45 * n((H, S))).astype(np.float32),
        "w2_words": w2_words, "w2_scales": w2_scales,
        "scale": np.random.uniform(0.4, 1.6, H).astype(np.float32),
        "stain": (0.5 * n(H)).astype(np.float32),
        "base": (0.6 * n(H)).astype(np.float32),
        "gain": (np.random.uniform(0.5, 2.0, H) * u[:, 0]).astype(np.float32),
        "w3": (0.3 * n((H, N)) / np.sqrt(H) / u).astype(np.float32),
    }


def reference(tab_words, tab_scales, offs, pos1, pos2, w1, focus, w2_words, w2_scales,
              scale, stain, base, gain, w3):
    v = unpack_weight(tab_words, tab_scales, "e4m3")[:, unstriped(offs)]
    h = (mxq(f64(w1), 0, "e4m3").T @ v) + f64(focus)
    g = unpack_weight(w2_words, w2_scales, "e2m1").T @ v
    a = np.exp(f64(scale)[:, None] * h[:, unstriped(pos1)] + f64(stain)[:, None])
    c = g[:, unstriped(pos2)] - f64(base)[:, None]
    y = c * a * f64(gain)[:, None]
    return np.tanh(mxq(f64(w3), 0, "e4m3").T @ mxq(y, 0, "e4m3"))

@@ -1,0 +1,290 @@
+from contextlib import ExitStack
+
+import concourse.mybir as mybir
+
+K, T, S, M, H, N = 1024, 2048, 1024, 512, 1024, 384
+FLOPS = 2 * (2 * K * H * S + H * N * M)
+
+F32 = mybir.dt.float32
+BF16 = mybir.dt.bfloat16
+I32 = mybir.dt.int32
+U32 = mybir.dt.uint32
+U16 = mybir.dt.uint16
+U8 = mybir.dt.uint8
+FP8X4 = mybir.dt.float8_e4m3fn_x4
+FP4X4 = mybir.dt.float4_e2m1fn_x4
+ACT = mybir.ActivationFunctionType
+ALU = mybir.AluOpType
+
+P = 128
+PACK = 4
+KP = P * PACK
+BANK = 512
+
+
+def tile_list_cast_review_scores_kernel(
+    tc, tab_words, tab_scales, offs, pos1, pos2, w1, focus, w2_words, w2_scales,
+    scale, stain, base, gain, w3, out,
+):
+    nc = tc.nc
+    with ExitStack() as ctx:
+        keep = ctx.enter_context(tc.tile_pool(name="keep", bufs=1))
+        ring = ctx.enter_context(tc.tile_pool(name="ring", bufs=4))
+        psum_h = ctx.enter_context(tc.psum_pool(name="psum_h", bufs=5))
+        psum_g = ctx.enter_context(tc.psum_pool(name="psum_g", bufs=3))
+
+        def held(name, shape, dtype):
+            return keep.tile(shape, dtype, name=name, align_bytes=64)
+
+        offs_t = keep.tile([P, S // 16], U16, name="offs_t")
+        pos1_t = keep.tile([P, M // 16], U16, name="pos1_t")
+        pos2_t = keep.tile([P, M // 16], U16, name="pos2_t")
+
+        tabs = held("tabs", [P, T], U8)
+        w2s_raw = held("w2s_raw", [P, 2 * H], U8)
+        vs1 = held("vs1", [P, S], U8)
+        nc.gpsimd.memset(tabs[:].bitcast(I32), 0)
+        nc.vector.memset(w2s_raw[:].bitcast(I32), 0)
+        nc.gpsimd.memset(vs1[:].bitcast(I32), 0)
+
+        tabw = [held(f"tabw{a}", [P, T], U32) for a in range(2)]
+        w2_raw = held("w2_raw", [P, 2, 2 * H], U8)
+        rows, w1_raw, w3_raw = {}, {}, {}
+        focus_t = [held(f"focus{b}", [P, PACK, S], F32) for b in range(2)]
+
+        def load_tab(a):
+            nc.sync.dma_start(tabw[a][:].bitcast(I32), tab_words[a].rearrange("p t i -> p (t i)").bitcast(I32))
+
+        def load_row(name, vec):
+            rows[name] = held("row_" + name, [P, 2 * PACK], F32)
+            nc.sync.dma_start(
+                rows[name][:].rearrange("p (b t) -> p b t", b=2), vec.rearrange("(b p t) -> p b t", b=2, t=PACK)
+            )
+
+        def load_w1(a, b):
+            w1_raw[a, b] = held(f"w1_raw{a}{b}", [P, PACK, KP], F32)
+            nc.sync.dma_start(
+                w1_raw[a, b][:],
+                w1[a * KP : (a + 1) * KP, b * KP : (b + 1) * KP].rearrange("(p j) c -> p j c", j=PACK),
+            )
+
+        def load_focus(b, t):
+            nc.sync.dma_start(
+                focus_t[b][:, t, :], focus[b * KP : (b + 1) * KP, :].rearrange("(p t) s -> p t s", t=PACK)[:, t, :]
+            )
+
+        def load_w3(b):
+            w3_raw[b] = held(f"w3_raw{b}", [P, PACK, N], F32)
+            nc.sync.dma_start(w3_raw[b][:], w3[b * KP : (b + 1) * KP, :].rearrange("(p j) n -> p j n", j=PACK))
+
+        nc.sync.dma_start(offs_t[:], offs)
+        for q in range(4):
+            (nc.scalar if q < 2 else nc.sync).dma_start(
+                tabs[32 * q : 32 * q + 8, :].bitcast(I32), tab_scales[:, 4 * q : 4 * q + 4, :].bitcast(I32)
+            )
+        nc.sync.dma_start(pos2_t[:], pos2)
+        load_tab(0)
+        nc.sync.dma_start(w2_raw[:].bitcast(I32), w2_words.rearrange("a p c -> p a c").bitcast(I32))
+        for q in range(4):
+            nc.sync.dma_start(
+                w2s_raw[32 * q : 32 * q + 4, :].bitcast(I32).rearrange("r (a c) -> r a c", a=2),
+                w2_scales[:, 4 * q : 4 * q + 4, :].bitcast(I32).rearrange("a r c -> r a c"),
+            )
+        load_tab(1)
+
+        vs0 = held("vs0", [P, S], U8)
+        nc.vector.tensor_copy(vs0[:], tabs[:].indirect(offs_t[:]))
+        nc.sync.dma_start(vs1[0:112, :].bitcast(I32), vs0[4:116, :].bitcast(I32))
+        vs = [vs0, vs1]
+
+        nc.sync.dma_start(pos1_t[:], pos1)
+        load_w1(0, 0)
+        load_w1(1, 0)
+        load_row("base", base)
+        load_row("gain", gain)
+        load_row("scale", scale)
+        load_row("stain", stain)
+        load_focus(0, 0)
+        load_focus(0, 1)
+        load_w1(0, 1)
+        load_focus(0, 2)
+        load_w1(1, 1)
+        load_focus(0, 3)
+        load_focus(1, 0)
+        load_w3(0)
+        load_focus(1, 1)
+        load_w3(1)
+        load_focus(1, 2)
+        load_focus(1, 3)
+
+        w2c = [held(f"w2c{b}", [P, 2, 2 * KP], U8) for b in range(2)]
+        w2s = [held(f"w2s{b}", [P, 2, KP], U8) for b in range(2)]
+        for b in range(2):
+            nc.scalar.copy(
+                w2c[b][:].bitcast(U16).rearrange("p a (t m) -> p a t m", t=PACK),
+                w2_raw[:].bitcast(U16)[:, :, b * KP : (b + 1) * KP].rearrange("p a (m t) -> p a t m", t=PACK),
+            )
+        vw = {}
+        vw0 = held("vw0", [P, S], U32)
+        nc.vector.tensor_copy(vw0[:], tabw[0][:].indirect(offs_t[:]))
+
+        def deal_w2_scales(b):
+            nc.vector.tensor_copy(
+                w2s[b][:].rearrange("p a (t m) -> p a t m", t=PACK),
+                w2s_raw[:].rearrange("p (a c) -> p a c", a=2)[:, :, b * KP : (b + 1) * KP].rearrange(
+                    "p a (m t) -> p a t m", t=PACK
+                ),
+            )
+
+        deal_w2_scales(0)
+        deal_w2_scales(1)
+        for half in range(2):
+            vw[0, half] = vw0[:, half * BANK : (half + 1) * BANK]
+            vw1 = held(f"vw1{half}", [P, BANK], U32)
+            nc.vector.tensor_copy(vw1[:], tabw[1][:].indirect(offs_t[:, half * 32 : (half + 1) * 32]))
+            vw[1, half] = vw1[:]
+
+        def first_stage(pool, codes, scales, half):
+            acc = pool.tile([P, BANK], F32, name="acc")
+            for a in range(2):
+                nc.tensor.matmul_mx(
+                    out=acc[:], lhsT=codes[a], lhsT_scale=scales[a],
+                    rhs=vw[a, half].bitcast(FP8X4), rhs_scale=vs[a][:, half * BANK : (half + 1) * BANK],
+                    start=(a == 0), stop=(a == 1),
+                )
+            return acc
+
+        c4 = [focus_t[b][:, :, 0:M] for b in range(2)]
+        a4 = [held(f"a4{b}", [P, PACK, M], F32) for b in range(2)]
+        g = {(b, t): held(f"g{b}{t}", [P, S], F32) for b in range(2) for t in range(PACK)}
+
+        def g_half(b, t, half):
+            acc = first_stage(
+                psum_g, [w2c[b][:, a, 2 * P * t : 2 * P * (t + 1)].bitcast(FP4X4) for a in range(2)],
+                [w2s[b][:, a, P * t : P * (t + 1)] for a in range(2)], half,
+            )
+            nc.scalar.copy(g[b, t][:, half * BANK : (half + 1) * BANK], acc[:])
+
+        def pick(b, t):
+            nc.vector.tensor_copy(c4[b][:, t, :], g[b, t][:].indirect(pos2_t[:]))
+
+        shift = held("shift", [P, 2 * PACK], F32)
+        nc.vector.scalar_tensor_tensor(shift[:], rows["base"][:], -1.0, rows["gain"][:], ALU.mult, ALU.mult)
+        def level(b, t):
+            col = slice(b * PACK + t, b * PACK + t + 1)
+            nc.scalar.activation(
+                out=c4[b][:, t, :], in_=c4[b][:, t, :], func=ACT.Identity, bias=shift[:, col], scale=rows["gain"][:, col]
+            )
+
+        w1c, w1s, w1g = {}, {}, {}
+
+        def rounding_copy(engine, dst, src):
+            if engine == "vector":
+                nc.vector.tensor_copy(dst, src)
+            elif engine == "gpsimd":
+                nc.gpsimd.tensor_scalar(dst, src, 1.0, 0.0, ALU.mult, ALU.add)
+            else:
+                nc.scalar.copy(dst, src)
+
+        def w1_round(a, b, engine):
+            w1g[a, b] = ring.tile([P, PACK * KP], BF16, name="grouped", align_bytes=64)
+            rounding_copy(
+                engine, w1g[a, b][:].rearrange("p (t m j) -> p m j t", t=PACK, j=PACK),
+                w1_raw[a, b][:].rearrange("p j (m t) -> p m j t", t=PACK),
+            )
+
+        def w1_quant(a, b):
+            w1c[a, b] = held(f"w1c{a}{b}", [P, KP], U32)
+            w1s[a, b] = held(f"w1s{a}{b}", [P, KP], U8)
+            nc.vector.quantize_mx(out=w1c[a, b][:].bitcast(FP8X4), scales=w1s[a, b][:], in_=w1g[a, b][:])
+
+        def h_tile(b, t):
+            h = ring.tile([P, S], F32, name="h")
+            for half in range(2):
+                cols = slice(half * BANK, (half + 1) * BANK)
+                acc = first_stage(
+                    psum_h, [w1c[a, b][:, P * t : P * (t + 1)].bitcast(FP8X4) for a in range(2)],
+                    [w1s[a, b][:, P * t : P * (t + 1)] for a in range(2)], half,
+                )
+                nc.vector.tensor_tensor(h[:, cols], acc[:], focus_t[b][:, t, cols], ALU.add)
+            col = slice(b * PACK + t, b * PACK + t + 1)
+            nc.scalar.activation(
+                out=a4[b][:, t, :], in_=h[:].indirect(pos1_t[:]), func=ACT.Exp,
+                bias=rows["stain"][:, col], scale=rows["scale"][:, col],
+            )
+
+        yg, yc, ys, w3g, w3c, w3s = {}, {}, {}, {}, {}, {}
+
+        def y_round(b):
+            yg[b] = ring.tile([P, PACK * M], BF16, name="grouped", align_bytes=64)
+            nc.vector.tensor_tensor(
+                yg[b][:].rearrange("p (c i t) -> p c t i", i=2, t=PACK),
+                c4[b].rearrange("p t (c i) -> p c t i", i=2),
+                a4[b][:].rearrange("p t (c i) -> p c t i", i=2),
+                ALU.mult,
+            )
+
+        def y_quant(b):
+            yc[b] = held(f"yc{b}", [P, M], U32)
+            ys[b] = held(f"ys{b}", [P, M], U8)
+            nc.vector.quantize_mx(out=yc[b][:].bitcast(FP8X4), scales=ys[b][:], in_=yg[b][:])
+
+        def w3_round(b, engine):
+            w3g[b] = held(f"w3g{b}", [P, PACK * N], BF16)
+            rounding_copy(
+                engine, w3g[b][:].rearrange("p (c i j) -> p c j i", i=4, j=PACK),
+                w3_raw[b][:].rearrange("p j (c i) -> p c j i", i=4),
+            )
+
+        def w3_quant(b):
+            w3c[b] = held(f"w3c{b}", [P, N], U32)
+            w3s[b] = held(f"w3s{b}", [P, N], U8)
+            nc.vector.quantize_mx(out=w3c[b][:].bitcast(FP8X4), scales=w3s[b][:], in_=w3g[b][:])
+
+        for t in range(2):
+            g_half(0, t, 0)
+        w1_round(0, 0, "vector")
+        w1_quant(0, 0)
+        w1_round(1, 0, "vector")
+        w1_quant(1, 0)
+        w1_round(0, 1, "scalar")
+        w1_round(1, 1, "scalar")
+        w1_quant(0, 1)
+        w1_quant(1, 1)
+        for t in range(2):
+            g_half(0, t, 1)
+        for t in range(2, PACK):
+            g_half(0, t, 0)
+            g_half(0, t, 1)
+        for t in range(PACK):
+            h_tile(0, t)
+            pick(0, t)
+            g_half(1, t, 0)
+            g_half(1, t, 1)
+        for t in range(PACK):
+            level(0, t)
+        w3_round(0, "scalar")
+        w3_quant(0)
+        w3_round(1, "vector")
+        w3_quant(1)
+        for t in range(PACK):
+            h_tile(1, t)
+            if t == 3:
+                y_round(0)
+                y_quant(0)
+            pick(1, t)
+            level(1, t)
+        y_round(1)
+        y_quant(1)
+
+        for i in range(N // P):
+            acc = psum_g.tile([P, M], F32, name="acc")
+            for b in range(2):
+                nc.tensor.matmul_mx(
+                    out=acc[:], lhsT=w3c[b][:, P * i : P * (i + 1)].bitcast(FP8X4),
+                    lhsT_scale=w3s[b][:, P * i : P * (i + 1)],
+                    rhs=yc[b][:].bitcast(FP8X4), rhs_scale=ys[b][:], start=(b == 0), stop=(b == 1),
+                )
+            res = held(f"res{i}", [P, M], F32)
+            nc.scalar.activation(out=res[:], in_=acc[:], func=ACT.Tanh)
+            nc.sync.dma_start(out[P * i : P * (i + 1), :], res[:])

@@ -29,12 +29,12 @@ def tile_list_cast_review_scores_kernel(
     nc = tc.nc
     with ExitStack() as ctx:
         keep = ctx.enter_context(tc.tile_pool(name="keep", bufs=1))
-        ring = ctx.enter_context(tc.tile_pool(name="ring", bufs=4))
+        ring = ctx.enter_context(tc.tile_pool(name="ring", bufs=3))
         psum_h = ctx.enter_context(tc.psum_pool(name="psum_h", bufs=5))
         psum_g = ctx.enter_context(tc.psum_pool(name="psum_g", bufs=3))
 
-        def held(name, shape, dtype):
-            return keep.tile(shape, dtype, name=name, align_bytes=64)
+        def held(name, shape, dtype, tag=None):
+            return keep.tile(shape, dtype, name=name, tag=tag or name, align_bytes=64)
 
         offs_t = keep.tile([P, S // 16], U16, name="offs_t")
         pos1_t = keep.tile([P, M // 16], U16, name="pos1_t")
@@ -45,36 +45,34 @@ def tile_list_cast_review_scores_kernel(
         vs1 = held("vs1", [P, S], U8)
         nc.gpsimd.memset(tabs[:].bitcast(I32), 0)
         nc.vector.memset(w2s_raw[:].bitcast(I32), 0)
-        nc.gpsimd.memset(vs1[:].bitcast(I32), 0)
+        nc.vector.memset(vs1[:].bitcast(I32), 0)
 
         tabw = [held(f"tabw{a}", [P, T], U32) for a in range(2)]
         w2_raw = held("w2_raw", [P, 2, 2 * H], U8)
-        rows, w1_raw, w3_raw = {}, {}, {}
+        w1_low = [held(f"w1_low{b}", [P, PACK, KP], F32) for b in range(2)]
+        w1_high = held("w1_high", [P, PACK, H], F32)
+        w1_raw = {(a, b): w1_high[:, :, b * KP : (b + 1) * KP] if a else w1_low[b][:] for a in range(2) for b in range(2)}
         focus_t = [held(f"focus{b}", [P, PACK, S], F32) for b in range(2)]
+        w3_raw = [held(f"w3_raw{b}", [P, PACK, N], F32) for b in range(2)]
 
         def load_tab(a):
             nc.sync.dma_start(tabw[a][:].bitcast(I32), tab_words[a].rearrange("p t i -> p (t i)").bitcast(I32))
 
         def load_row(name, vec):
-            rows[name] = held("row_" + name, [P, 2 * PACK], F32)
-            nc.sync.dma_start(
-                rows[name][:].rearrange("p (b t) -> p b t", b=2), vec.rearrange("(b p t) -> p b t", b=2, t=PACK)
-            )
+            row = held(name, [P, 2, 2 * PACK], F32)
+            nc.gpsimd.dma_start(row[:, :, 0:PACK], vec.rearrange("(b p t) -> p b t", b=2, t=PACK))
+            return row
 
-        def load_w1(a, b):
-            w1_raw[a, b] = held(f"w1_raw{a}{b}", [P, PACK, KP], F32)
-            nc.sync.dma_start(
-                w1_raw[a, b][:],
-                w1[a * KP : (a + 1) * KP, b * KP : (b + 1) * KP].rearrange("(p j) c -> p j c", j=PACK),
-            )
+        def load_w1(dst, a, cols):
+            nc.sync.dma_start(dst[:], w1[a * KP : (a + 1) * KP, cols].rearrange("(p j) c -> p j c", j=PACK))
 
-        def load_focus(b, t):
+        def load_focus(b, slots):
             nc.sync.dma_start(
-                focus_t[b][:, t, :], focus[b * KP : (b + 1) * KP, :].rearrange("(p t) s -> p t s", t=PACK)[:, t, :]
+                focus_t[b][:, slots, :],
+                focus[b * KP : (b + 1) * KP, :].rearrange("(p t) s -> p t s", t=PACK)[:, slots, :],
             )
 
         def load_w3(b):
-            w3_raw[b] = held(f"w3_raw{b}", [P, PACK, N], F32)
             nc.sync.dma_start(w3_raw[b][:], w3[b * KP : (b + 1) * KP, :].rearrange("(p j) n -> p j n", j=PACK))
 
         nc.sync.dma_start(offs_t[:], offs)
@@ -96,26 +94,20 @@ def tile_list_cast_review_scores_kernel(
         nc.vector.tensor_copy(vs0[:], tabs[:].indirect(offs_t[:]))
         nc.sync.dma_start(vs1[0:112, :].bitcast(I32), vs0[4:116, :].bitcast(I32))
         vs = [vs0, vs1]
-
+        scale_t = load_row("scale_t", scale)
+        stain_t = load_row("stain_t", stain)
+        base_t = load_row("base_t", base)
+        gain_t = load_row("gain_t", gain)
+        load_w1(w1_low[0], 0, slice(0, KP))
+        load_w1(w1_high, 1, slice(0, H))
+        load_w1(w1_low[1], 0, slice(KP, H))
         nc.sync.dma_start(pos1_t[:], pos1)
-        load_w1(0, 0)
-        load_w1(1, 0)
-        load_row("base", base)
-        load_row("gain", gain)
-        load_row("scale", scale)
-        load_row("stain", stain)
-        load_focus(0, 0)
-        load_focus(0, 1)
-        load_w1(0, 1)
-        load_focus(0, 2)
-        load_w1(1, 1)
-        load_focus(0, 3)
-        load_focus(1, 0)
+        for t in range(PACK):
+            load_focus(0, slice(t, t + 1))
+        for t in range(PACK):
+            load_focus(1, slice(t, t + 1))
         load_w3(0)
-        load_focus(1, 1)
         load_w3(1)
-        load_focus(1, 2)
-        load_focus(1, 3)
 
         w2c = [held(f"w2c{b}", [P, 2, 2 * KP], U8) for b in range(2)]
         w2s = [held(f"w2s{b}", [P, 2, KP], U8) for b in range(2)]
@@ -124,20 +116,16 @@ def tile_list_cast_review_scores_kernel(
                 w2c[b][:].bitcast(U16).rearrange("p a (t m) -> p a t m", t=PACK),
                 w2_raw[:].bitcast(U16)[:, :, b * KP : (b + 1) * KP].rearrange("p a (m t) -> p a t m", t=PACK),
             )
-        vw = {}
         vw0 = held("vw0", [P, S], U32)
         nc.vector.tensor_copy(vw0[:], tabw[0][:].indirect(offs_t[:]))
-
-        def deal_w2_scales(b):
+        for b in range(2):
             nc.vector.tensor_copy(
                 w2s[b][:].rearrange("p a (t m) -> p a t m", t=PACK),
                 w2s_raw[:].rearrange("p (a c) -> p a c", a=2)[:, :, b * KP : (b + 1) * KP].rearrange(
                     "p a (m t) -> p a t m", t=PACK
                 ),
             )
-
-        deal_w2_scales(0)
-        deal_w2_scales(1)
+        vw = {}
         for half in range(2):
             vw[0, half] = vw0[:, half * BANK : (half + 1) * BANK]
             vw1 = held(f"vw1{half}", [P, BANK], U32)
@@ -154,9 +142,11 @@ def tile_list_cast_review_scores_kernel(
                 )
             return acc
 
-        c4 = [focus_t[b][:, :, 0:M] for b in range(2)]
-        a4 = [held(f"a4{b}", [P, PACK, M], F32) for b in range(2)]
+        picked = [w1_raw[0, 0], focus_t[1][:, :, 0:M]]
+        leveled = [focus_t[0][:, :, 0:M], focus_t[1][:, :, 0:M]]
+        looked = [w1_raw[1, 1], held("looked1", [P, PACK, M], F32)[:]]
         g = {(b, t): held(f"g{b}{t}", [P, S], F32) for b in range(2) for t in range(PACK)}
+        h = {}
 
         def g_half(b, t, half):
             acc = first_stage(
@@ -166,31 +156,25 @@ def tile_list_cast_review_scores_kernel(
             nc.scalar.copy(g[b, t][:, half * BANK : (half + 1) * BANK], acc[:])
 
         def pick(b, t):
-            nc.vector.tensor_copy(c4[b][:, t, :], g[b, t][:].indirect(pos2_t[:]))
+            nc.vector.tensor_copy(picked[b][:, t, :], g[b, t][:].indirect(pos2_t[:]))
 
-        shift = held("shift", [P, 2 * PACK], F32)
-        nc.vector.scalar_tensor_tensor(shift[:], rows["base"][:], -1.0, rows["gain"][:], ALU.mult, ALU.mult)
+        shift = held("shift", [P, 2, PACK], F32)
+        nc.gpsimd.tensor_tensor(shift[:], base_t[:, :, 0:PACK], gain_t[:, :, 0:PACK], ALU.mult)
+        nc.gpsimd.tensor_scalar(shift[:], shift[:], -1.0, 0.0, ALU.mult, ALU.add)
+
         def level(b, t):
-            col = slice(b * PACK + t, b * PACK + t + 1)
-            nc.scalar.activation(
-                out=c4[b][:, t, :], in_=c4[b][:, t, :], func=ACT.Identity, bias=shift[:, col], scale=rows["gain"][:, col]
+            nc.gpsimd.tensor_scalar(
+                leveled[b][:, t, :], picked[b][:, t, :], gain_t[:, b, t : t + 1], shift[:, b, t : t + 1],
+                ALU.mult, ALU.add,
             )
 
         w1c, w1s, w1g = {}, {}, {}
 
-        def rounding_copy(engine, dst, src):
-            if engine == "vector":
-                nc.vector.tensor_copy(dst, src)
-            elif engine == "gpsimd":
-                nc.gpsimd.tensor_scalar(dst, src, 1.0, 0.0, ALU.mult, ALU.add)
-            else:
-                nc.scalar.copy(dst, src)
-
-        def w1_round(a, b, engine):
-            w1g[a, b] = ring.tile([P, PACK * KP], BF16, name="grouped", align_bytes=64)
-            rounding_copy(
-                engine, w1g[a, b][:].rearrange("p (t m j) -> p m j t", t=PACK, j=PACK),
-                w1_raw[a, b][:].rearrange("p j (m t) -> p m j t", t=PACK),
+        def w1_round(a, b, copy):
+            w1g[a, b] = ring.tile([P, PACK * KP], BF16, name="w1g", align_bytes=64)
+            copy(
+                w1g[a, b][:].rearrange("p (t m j) -> p m j t", t=PACK, j=PACK),
+                w1_raw[a, b].rearrange("p j (m t) -> p m j t", t=PACK),
             )
 
         def w1_quant(a, b):
@@ -199,92 +183,101 @@ def tile_list_cast_review_scores_kernel(
             nc.vector.quantize_mx(out=w1c[a, b][:].bitcast(FP8X4), scales=w1s[a, b][:], in_=w1g[a, b][:])
 
         def h_tile(b, t):
-            h = ring.tile([P, S], F32, name="h")
+            h[b, t] = held(f"h{b}{t}", [P, S], F32)
             for half in range(2):
                 cols = slice(half * BANK, (half + 1) * BANK)
                 acc = first_stage(
                     psum_h, [w1c[a, b][:, P * t : P * (t + 1)].bitcast(FP8X4) for a in range(2)],
                     [w1s[a, b][:, P * t : P * (t + 1)] for a in range(2)], half,
                 )
-                nc.vector.tensor_tensor(h[:, cols], acc[:], focus_t[b][:, t, cols], ALU.add)
-            col = slice(b * PACK + t, b * PACK + t + 1)
+                nc.vector.tensor_tensor(h[b, t][:, cols], acc[:], focus_t[b][:, t, cols], ALU.add)
+
+        def look(b, t):
             nc.scalar.activation(
-                out=a4[b][:, t, :], in_=h[:].indirect(pos1_t[:]), func=ACT.Exp,
-                bias=rows["stain"][:, col], scale=rows["scale"][:, col],
+                out=looked[b][:, t, :], in_=h[b, t][:].indirect(pos1_t[:]), func=ACT.Exp,
+                bias=stain_t[:, b, t : t + 1], scale=scale_t[:, b, t : t + 1],
             )
 
-        yg, yc, ys, w3g, w3c, w3s = {}, {}, {}, {}, {}, {}
+        yg, w3g, w3c, w3s = {}, {}, {}, {}
+        yc = [held(f"yc{b}", [P, M], U32) for b in range(2)]
+        ys = [held(f"ys{b}", [P, M], U8) for b in range(2)]
 
-        def y_round(b):
-            yg[b] = ring.tile([P, PACK * M], BF16, name="grouped", align_bytes=64)
+        def y_round(b, cols, tag):
+            yg[b, cols.start] = held("yg", [P, PACK * (cols.stop - cols.start)], BF16, tag)
             nc.vector.tensor_tensor(
-                yg[b][:].rearrange("p (c i t) -> p c t i", i=2, t=PACK),
-                c4[b].rearrange("p t (c i) -> p c t i", i=2),
-                a4[b][:].rearrange("p t (c i) -> p c t i", i=2),
+                yg[b, cols.start][:].rearrange("p (c i t) -> p c t i", i=4, t=PACK),
+                leveled[b][:, :, cols].rearrange("p t (c i) -> p c t i", i=4),
+                looked[b][:, :, cols].rearrange("p t (c i) -> p c t i", i=4),
                 ALU.mult,
             )
 
-        def y_quant(b):
-            yc[b] = held(f"yc{b}", [P, M], U32)
-            ys[b] = held(f"ys{b}", [P, M], U8)
-            nc.vector.quantize_mx(out=yc[b][:].bitcast(FP8X4), scales=ys[b][:], in_=yg[b][:])
+        def y_quant(b, cols):
+            nc.vector.quantize_mx(out=yc[b][:, cols].bitcast(FP8X4), scales=ys[b][:, cols], in_=yg[b, cols.start][:])
 
-        def w3_round(b, engine):
-            w3g[b] = held(f"w3g{b}", [P, PACK * N], BF16)
-            rounding_copy(
-                engine, w3g[b][:].rearrange("p (c i j) -> p c j i", i=4, j=PACK),
+        def w3_round(b):
+            w3g[b] = held("w3g", [P, PACK * N], BF16, f"h1{b + 2}")
+            nc.scalar.copy(
+                w3g[b][:].rearrange("p (c i j) -> p c j i", i=4, j=PACK),
                 w3_raw[b][:].rearrange("p j (c i) -> p c j i", i=4),
             )
 
-        def w3_quant(b):
-            w3c[b] = held(f"w3c{b}", [P, N], U32)
+        def w3_quant(b, tag):
+            w3c[b] = held("w3c", [P, N], U32, tag)
             w3s[b] = held(f"w3s{b}", [P, N], U8)
             nc.vector.quantize_mx(out=w3c[b][:].bitcast(FP8X4), scales=w3s[b][:], in_=w3g[b][:])
 
+        def scores(pool, cols):
+            width = cols.stop - cols.start
+            for i in range(N // P):
+                acc = pool.tile([P, BANK], F32, name="acc")
+                for b in range(2):
+                    nc.tensor.matmul_mx(
+                        out=acc[:, 0:width], lhsT=w3c[b][:, P * i : P * (i + 1)].bitcast(FP8X4),
+                        lhsT_scale=w3s[b][:, P * i : P * (i + 1)],
+                        rhs=yc[b][:, cols].bitcast(FP8X4), rhs_scale=ys[b][:, cols], start=(b == 0), stop=(b == 1),
+                    )
+                res = held(f"res{i}_{cols.start}", [P, width], F32)
+                nc.scalar.activation(out=res[:], in_=acc[:, 0:width], func=ACT.Tanh)
+                nc.sync.dma_start(out[P * i : P * (i + 1), cols], res[:])
+
         for t in range(2):
             g_half(0, t, 0)
-        w1_round(0, 0, "vector")
+        w1_round(0, 0, nc.vector.tensor_copy)
         w1_quant(0, 0)
-        w1_round(1, 0, "vector")
+        w1_round(1, 0, nc.vector.tensor_copy)
         w1_quant(1, 0)
-        w1_round(0, 1, "scalar")
-        w1_round(1, 1, "scalar")
-        w1_quant(0, 1)
-        w1_quant(1, 1)
         for t in range(2):
             g_half(0, t, 1)
         for t in range(2, PACK):
             g_half(0, t, 0)
             g_half(0, t, 1)
+        w1_round(1, 1, nc.scalar.copy)
+        w1_round(0, 1, nc.scalar.copy)
+        w1_quant(1, 1)
+        w1_quant(0, 1)
         for t in range(PACK):
-            h_tile(0, t)
-            pick(0, t)
             g_half(1, t, 0)
             g_half(1, t, 1)
+            h_tile(0, t)
+            look(0, t)
         for t in range(PACK):
+            pick(0, t)
             level(0, t)
-        w3_round(0, "scalar")
-        w3_quant(0)
-        w3_round(1, "vector")
-        w3_quant(1)
         for t in range(PACK):
             h_tile(1, t)
-            if t == 3:
-                y_round(0)
-                y_quant(0)
+            look(1, t)
             pick(1, t)
             level(1, t)
-        y_round(1)
-        y_quant(1)
-
-        for i in range(N // P):
-            acc = psum_g.tile([P, M], F32, name="acc")
-            for b in range(2):
-                nc.tensor.matmul_mx(
-                    out=acc[:], lhsT=w3c[b][:, P * i : P * (i + 1)].bitcast(FP8X4),
-                    lhsT_scale=w3s[b][:, P * i : P * (i + 1)],
-                    rhs=yc[b][:].bitcast(FP8X4), rhs_scale=ys[b][:], start=(b == 0), stop=(b == 1),
-                )
-            res = held(f"res{i}", [P, M], F32)
-            nc.scalar.activation(out=res[:], in_=acc[:], func=ACT.Tanh)
-            nc.sync.dma_start(out[P * i : P * (i + 1), :], res[:])
+        w3_round(0)
+        w3_round(1)
+        halves = [slice(0, M // 2), slice(M // 2, M)]
+        y_round(0, slice(0, M), "g13")
+        w3_quant(0, "w1_high")
+        y_quant(0, slice(0, M))
+        y_round(1, halves[0], "focus0")
+        w3_quant(1, "g13")
+        y_quant(1, halves[0])
+        y_round(1, halves[1], "focus0")
+        y_quant(1, halves[1])
+        scores(psum_g, halves[0])
+        scores(psum_h, halves[1])

@@ -20,6 +20,11 @@ P = 128
 PACK = 4
 KP = P * PACK
 BANK = 512
+GROUP = 16
+QUADRANTS = 4
+LAST_SCALE_ROW = 32 * (QUADRANTS - 1) + PACK
+H_BANKS = 5
+G_BANKS = 3
 
 
 def tile_list_cast_review_scores_kernel(
@@ -30,128 +35,124 @@ def tile_list_cast_review_scores_kernel(
     with ExitStack() as ctx:
         keep = ctx.enter_context(tc.tile_pool(name="keep", bufs=1))
         ring = ctx.enter_context(tc.tile_pool(name="ring", bufs=3))
-        psum_h = ctx.enter_context(tc.psum_pool(name="psum_h", bufs=5))
-        psum_g = ctx.enter_context(tc.psum_pool(name="psum_g", bufs=3))
+        psum_h = ctx.enter_context(tc.psum_pool(name="psum_h", bufs=H_BANKS))
+        psum_g = ctx.enter_context(tc.psum_pool(name="psum_g", bufs=G_BANKS))
 
-        def held(name, shape, dtype, tag=None):
-            return keep.tile(shape, dtype, name=name, tag=tag or name, align_bytes=64)
+        def held(name, shape, dtype, reuses=None):
+            return keep.tile(shape, dtype, name=name, tag=reuses or name, align_bytes=64)
 
-        offs_t = keep.tile([P, S // 16], U16, name="offs_t")
-        pos1_t = keep.tile([P, M // 16], U16, name="pos1_t")
-        pos2_t = keep.tile([P, M // 16], U16, name="pos2_t")
+        offs_t = keep.tile([P, S // GROUP], U16, name="offs_t")
+        pos1_t = keep.tile([P, M // GROUP], U16, name="pos1_t")
+        pos2_t = keep.tile([P, M // GROUP], U16, name="pos2_t")
 
-        tabs = held("tabs", [P, T], U8)
-        w2s_raw = held("w2s_raw", [P, 2 * H], U8)
-        vs1 = held("vs1", [P, S], U8)
-        nc.gpsimd.memset(tabs[:].bitcast(I32), 0)
-        nc.vector.memset(w2s_raw[:].bitcast(I32), 0)
-        nc.vector.memset(vs1[:].bitcast(I32), 0)
+        tab_s = held("tab_s", [P, T], U8)
+        w2_s_raw = held("w2_s_raw", [P, 2 * H], U8)
+        v_s1 = held("v_s1", [P, S], U8)
+        nc.gpsimd.memset(tab_s[:].bitcast(I32), 0)
+        nc.vector.memset(w2_s_raw[:].bitcast(I32), 0)
+        nc.vector.memset(v_s1[32 * (QUADRANTS - 1) :, :].bitcast(I32), 0)
 
-        tabw = [held(f"tabw{a}", [P, T], U32) for a in range(2)]
-        w2_raw = held("w2_raw", [P, 2, 2 * H], U8)
+        tab_w = [held(f"tab_w{a}", [P, T], U32) for a in range(2)]
+        w2_w_raw = held("w2_w_raw", [P, 2, 2 * H], U8)
         w1_low = [held(f"w1_low{b}", [P, PACK, KP], F32) for b in range(2)]
         w1_high = held("w1_high", [P, PACK, H], F32)
-        w1_raw = {(a, b): w1_high[:, :, b * KP : (b + 1) * KP] if a else w1_low[b][:] for a in range(2) for b in range(2)}
+        w1_raw = {
+            (a, b): w1_high[:, :, b * KP : (b + 1) * KP] if a else w1_low[b][:] for a in range(2) for b in range(2)
+        }
         focus_t = [held(f"focus{b}", [P, PACK, S], F32) for b in range(2)]
         w3_raw = [held(f"w3_raw{b}", [P, PACK, N], F32) for b in range(2)]
 
-        def load_tab(a):
-            nc.sync.dma_start(tabw[a][:].bitcast(I32), tab_words[a].rearrange("p t i -> p (t i)").bitcast(I32))
+        def load_tab_words(a):
+            nc.sync.dma_start(tab_w[a][:].bitcast(I32), tab_words[a].rearrange("p t i -> p (t i)").bitcast(I32))
 
-        def load_row(name, vec):
-            row = held(name, [P, 2, 2 * PACK], F32)
-            nc.gpsimd.dma_start(row[:, :, 0:PACK], vec.rearrange("(b p t) -> p b t", b=2, t=PACK))
-            return row
+        def load_row_values(name, vec):
+            values = held(name, [P, 2, 2 * PACK], F32)
+            nc.gpsimd.dma_start(values[:, :, 0:PACK], vec.rearrange("(b p t) -> p b t", b=2, t=PACK))
+            return values
 
         def load_w1(dst, a, cols):
             nc.sync.dma_start(dst[:], w1[a * KP : (a + 1) * KP, cols].rearrange("(p j) c -> p j c", j=PACK))
 
-        def load_focus(b, slots):
-            nc.sync.dma_start(
-                focus_t[b][:, slots, :],
-                focus[b * KP : (b + 1) * KP, :].rearrange("(p t) s -> p t s", t=PACK)[:, slots, :],
-            )
-
-        def load_w3(b):
-            nc.sync.dma_start(w3_raw[b][:], w3[b * KP : (b + 1) * KP, :].rearrange("(p j) n -> p j n", j=PACK))
-
         nc.sync.dma_start(offs_t[:], offs)
-        for q in range(4):
-            (nc.scalar if q < 2 else nc.sync).dma_start(
-                tabs[32 * q : 32 * q + 8, :].bitcast(I32), tab_scales[:, 4 * q : 4 * q + 4, :].bitcast(I32)
+        for q in range(QUADRANTS):
+            (nc.scalar if q < QUADRANTS // 2 else nc.sync).dma_start(
+                tab_s[32 * q : 32 * q + 2 * PACK, :].bitcast(I32),
+                tab_scales[:, PACK * q : PACK * (q + 1), :].bitcast(I32),
             )
         nc.sync.dma_start(pos2_t[:], pos2)
-        load_tab(0)
-        nc.sync.dma_start(w2_raw[:].bitcast(I32), w2_words.rearrange("a p c -> p a c").bitcast(I32))
-        for q in range(4):
+        load_tab_words(0)
+        nc.sync.dma_start(w2_w_raw[:].bitcast(I32), w2_words.rearrange("a p c -> p a c").bitcast(I32))
+        for q in range(QUADRANTS):
             nc.sync.dma_start(
-                w2s_raw[32 * q : 32 * q + 4, :].bitcast(I32).rearrange("r (a c) -> r a c", a=2),
-                w2_scales[:, 4 * q : 4 * q + 4, :].bitcast(I32).rearrange("a r c -> r a c"),
+                w2_s_raw[32 * q : 32 * q + PACK, :].bitcast(I32).rearrange("r (a c) -> r a c", a=2),
+                w2_scales[:, PACK * q : PACK * (q + 1), :].bitcast(I32).rearrange("a r c -> r a c"),
             )
-        load_tab(1)
+        load_tab_words(1)
 
-        vs0 = held("vs0", [P, S], U8)
-        nc.vector.tensor_copy(vs0[:], tabs[:].indirect(offs_t[:]))
-        nc.sync.dma_start(vs1[0:112, :].bitcast(I32), vs0[4:116, :].bitcast(I32))
-        vs = [vs0, vs1]
-        scale_t = load_row("scale_t", scale)
-        stain_t = load_row("stain_t", stain)
-        base_t = load_row("base_t", base)
-        gain_t = load_row("gain_t", gain)
+        v_s0 = held("v_s0", [P, S], U8)
+        nc.vector.tensor_copy(v_s0[:], tab_s[:].indirect(offs_t[:]))
+        nc.sync.dma_start(v_s1[0:LAST_SCALE_ROW, :].bitcast(I32), v_s0[PACK : PACK + LAST_SCALE_ROW, :].bitcast(I32))
+        v_s = [v_s0, v_s1]
+
+        scale_t = load_row_values("scale_t", scale)
+        stain_t = load_row_values("stain_t", stain)
+        base_t = load_row_values("base_t", base)
+        gain_t = load_row_values("gain_t", gain)
         load_w1(w1_low[0], 0, slice(0, KP))
         load_w1(w1_high, 1, slice(0, H))
         load_w1(w1_low[1], 0, slice(KP, H))
         nc.sync.dma_start(pos1_t[:], pos1)
-        for t in range(PACK):
-            load_focus(0, slice(t, t + 1))
-        for t in range(PACK):
-            load_focus(1, slice(t, t + 1))
-        load_w3(0)
-        load_w3(1)
+        for b in range(2):
+            rows = focus[b * KP : (b + 1) * KP, :].rearrange("(p t) s -> p t s", t=PACK)
+            for t in range(PACK):
+                nc.sync.dma_start(focus_t[b][:, t : t + 1, :], rows[:, t : t + 1, :])
+        for b in range(2):
+            nc.sync.dma_start(w3_raw[b][:], w3[b * KP : (b + 1) * KP, :].rearrange("(p j) n -> p j n", j=PACK))
 
-        w2c = [held(f"w2c{b}", [P, 2, 2 * KP], U8) for b in range(2)]
-        w2s = [held(f"w2s{b}", [P, 2, KP], U8) for b in range(2)]
+        w2_w = [held(f"w2_w{b}", [P, 2, 2 * KP], U8) for b in range(2)]
+        w2_s = [held(f"w2_s{b}", [P, 2, KP], U8) for b in range(2)]
         for b in range(2):
             nc.scalar.copy(
-                w2c[b][:].bitcast(U16).rearrange("p a (t m) -> p a t m", t=PACK),
-                w2_raw[:].bitcast(U16)[:, :, b * KP : (b + 1) * KP].rearrange("p a (m t) -> p a t m", t=PACK),
+                w2_w[b][:].bitcast(U16).rearrange("p a (t m) -> p a t m", t=PACK),
+                w2_w_raw[:].bitcast(U16)[:, :, b * KP : (b + 1) * KP].rearrange("p a (m t) -> p a t m", t=PACK),
             )
-        vw0 = held("vw0", [P, S], U32)
-        nc.vector.tensor_copy(vw0[:], tabw[0][:].indirect(offs_t[:]))
+        v_w0 = held("v_w0", [P, S], U32)
+        nc.vector.tensor_copy(v_w0[:], tab_w[0][:].indirect(offs_t[:]))
         for b in range(2):
             nc.vector.tensor_copy(
-                w2s[b][:].rearrange("p a (t m) -> p a t m", t=PACK),
-                w2s_raw[:].rearrange("p (a c) -> p a c", a=2)[:, :, b * KP : (b + 1) * KP].rearrange(
+                w2_s[b][:].rearrange("p a (t m) -> p a t m", t=PACK),
+                w2_s_raw[:].rearrange("p (a c) -> p a c", a=2)[:, :, b * KP : (b + 1) * KP].rearrange(
                     "p a (m t) -> p a t m", t=PACK
                 ),
             )
-        vw = {}
-        for half in range(2):
-            vw[0, half] = vw0[:, half * BANK : (half + 1) * BANK]
-            vw1 = held(f"vw1{half}", [P, BANK], U32)
-            nc.vector.tensor_copy(vw1[:], tabw[1][:].indirect(offs_t[:, half * 32 : (half + 1) * 32]))
-            vw[1, half] = vw1[:]
+        v_w = {}
+        for half in range(S // BANK):
+            v_w[0, half] = v_w0[:, half * BANK : (half + 1) * BANK]
+            v_w1 = held(f"v_w1{half}", [P, BANK], U32)
+            entries = offs_t[:, half * BANK // GROUP : (half + 1) * BANK // GROUP]
+            nc.vector.tensor_copy(v_w1[:], tab_w[1][:].indirect(entries))
+            v_w[1, half] = v_w1[:]
 
         def first_stage(pool, codes, scales, half):
             acc = pool.tile([P, BANK], F32, name="acc")
             for a in range(2):
                 nc.tensor.matmul_mx(
                     out=acc[:], lhsT=codes[a], lhsT_scale=scales[a],
-                    rhs=vw[a, half].bitcast(FP8X4), rhs_scale=vs[a][:, half * BANK : (half + 1) * BANK],
+                    rhs=v_w[a, half].bitcast(FP8X4), rhs_scale=v_s[a][:, half * BANK : (half + 1) * BANK],
                     start=(a == 0), stop=(a == 1),
                 )
             return acc
 
         picked = [w1_raw[0, 0], focus_t[1][:, :, 0:M]]
-        leveled = [focus_t[0][:, :, 0:M], focus_t[1][:, :, 0:M]]
+        levelled = [focus_t[0][:, :, 0:M], focus_t[1][:, :, 0:M]]
         looked = [w1_raw[1, 1], held("looked1", [P, PACK, M], F32)[:]]
         g = {(b, t): held(f"g{b}{t}", [P, S], F32) for b in range(2) for t in range(PACK)}
         h = {}
 
         def g_half(b, t, half):
             acc = first_stage(
-                psum_g, [w2c[b][:, a, 2 * P * t : 2 * P * (t + 1)].bitcast(FP4X4) for a in range(2)],
-                [w2s[b][:, a, P * t : P * (t + 1)] for a in range(2)], half,
+                psum_g, [w2_w[b][:, a, 2 * P * t : 2 * P * (t + 1)].bitcast(FP4X4) for a in range(2)],
+                [w2_s[b][:, a, P * t : P * (t + 1)] for a in range(2)], half,
             )
             nc.scalar.copy(g[b, t][:, half * BANK : (half + 1) * BANK], acc[:])
 
@@ -163,32 +164,35 @@ def tile_list_cast_review_scores_kernel(
         nc.gpsimd.tensor_scalar(shift[:], shift[:], -1.0, 0.0, ALU.mult, ALU.add)
 
         def level(b, t):
-            nc.gpsimd.tensor_scalar(
-                leveled[b][:, t, :], picked[b][:, t, :], gain_t[:, b, t : t + 1], shift[:, b, t : t + 1],
-                ALU.mult, ALU.add,
-            )
+            factor, offset = gain_t[:, b, t : t + 1], shift[:, b, t : t + 1]
+            if (b, t) == (1, PACK - 1):
+                nc.scalar.activation(
+                    out=levelled[b][:, t, :], in_=picked[b][:, t, :], func=ACT.Identity, bias=offset, scale=factor
+                )
+            else:
+                nc.gpsimd.tensor_scalar(levelled[b][:, t, :], picked[b][:, t, :], factor, offset, ALU.mult, ALU.add)
 
-        w1c, w1s, w1g = {}, {}, {}
+        w1_bf, w1_w, w1_s = {}, {}, {}
 
         def w1_round(a, b, copy):
-            w1g[a, b] = ring.tile([P, PACK * KP], BF16, name="w1g", align_bytes=64)
+            w1_bf[a, b] = ring.tile([P, PACK * KP], BF16, name="w1_bf", align_bytes=64)
             copy(
-                w1g[a, b][:].rearrange("p (t m j) -> p m j t", t=PACK, j=PACK),
-                w1_raw[a, b].rearrange("p j (m t) -> p m j t", t=PACK),
+                w1_bf[a, b][:].rearrange("p (u e m j) -> p u m j e", u=2, e=2, j=PACK),
+                w1_raw[a, b].rearrange("p j (m u e) -> p u m j e", u=2, e=2),
             )
 
         def w1_quant(a, b):
-            w1c[a, b] = held(f"w1c{a}{b}", [P, KP], U32)
-            w1s[a, b] = held(f"w1s{a}{b}", [P, KP], U8)
-            nc.vector.quantize_mx(out=w1c[a, b][:].bitcast(FP8X4), scales=w1s[a, b][:], in_=w1g[a, b][:])
+            w1_w[a, b] = held(f"w1_w{a}{b}", [P, KP], U32)
+            w1_s[a, b] = held(f"w1_s{a}{b}", [P, KP], U8)
+            nc.vector.quantize_mx(out=w1_w[a, b][:].bitcast(FP8X4), scales=w1_s[a, b][:], in_=w1_bf[a, b][:])
 
         def h_tile(b, t):
             h[b, t] = held(f"h{b}{t}", [P, S], F32)
-            for half in range(2):
+            for half in range(S // BANK):
                 cols = slice(half * BANK, (half + 1) * BANK)
                 acc = first_stage(
-                    psum_h, [w1c[a, b][:, P * t : P * (t + 1)].bitcast(FP8X4) for a in range(2)],
-                    [w1s[a, b][:, P * t : P * (t + 1)] for a in range(2)], half,
+                    psum_h, [w1_w[a, b][:, P * t : P * (t + 1)].bitcast(FP8X4) for a in range(2)],
+                    [w1_s[a, b][:, P * t : P * (t + 1)] for a in range(2)], half,
                 )
                 nc.vector.tensor_tensor(h[b, t][:, cols], acc[:], focus_t[b][:, t, cols], ALU.add)
 
@@ -198,33 +202,35 @@ def tile_list_cast_review_scores_kernel(
                 bias=stain_t[:, b, t : t + 1], scale=scale_t[:, b, t : t + 1],
             )
 
-        yg, w3g, w3c, w3s = {}, {}, {}, {}
-        yc = [held(f"yc{b}", [P, M], U32) for b in range(2)]
-        ys = [held(f"ys{b}", [P, M], U8) for b in range(2)]
+        y_bf, w3_bf, w3_w, w3_s = {}, {}, {}, {}
+        y_w = [held(f"y_w{b}", [P, M], U32) for b in range(2)]
+        y_s = [held(f"y_s{b}", [P, M], U8) for b in range(2)]
 
-        def y_round(b, cols, tag):
-            yg[b, cols.start] = held("yg", [P, PACK * (cols.stop - cols.start)], BF16, tag)
+        def y_round(b, cols, reuses):
+            y_bf[b, cols.start] = held("y_bf", [P, PACK * (cols.stop - cols.start)], BF16, reuses)
             nc.vector.tensor_tensor(
-                yg[b, cols.start][:].rearrange("p (c i t) -> p c t i", i=4, t=PACK),
-                leveled[b][:, :, cols].rearrange("p t (c i) -> p c t i", i=4),
+                y_bf[b, cols.start][:].rearrange("p (c i t) -> p c t i", i=4, t=PACK),
+                levelled[b][:, :, cols].rearrange("p t (c i) -> p c t i", i=4),
                 looked[b][:, :, cols].rearrange("p t (c i) -> p c t i", i=4),
                 ALU.mult,
             )
 
         def y_quant(b, cols):
-            nc.vector.quantize_mx(out=yc[b][:, cols].bitcast(FP8X4), scales=ys[b][:, cols], in_=yg[b, cols.start][:])
+            nc.vector.quantize_mx(
+                out=y_w[b][:, cols].bitcast(FP8X4), scales=y_s[b][:, cols], in_=y_bf[b, cols.start][:]
+            )
 
-        def w3_round(b):
-            w3g[b] = held("w3g", [P, PACK * N], BF16, f"h1{b + 2}")
+        def w3_round(b, reuses):
+            w3_bf[b] = held("w3_bf", [P, PACK * N], BF16, reuses)
             nc.scalar.copy(
-                w3g[b][:].rearrange("p (c i j) -> p c j i", i=4, j=PACK),
+                w3_bf[b][:].rearrange("p (c i j) -> p c j i", i=4, j=PACK),
                 w3_raw[b][:].rearrange("p j (c i) -> p c j i", i=4),
             )
 
-        def w3_quant(b, tag):
-            w3c[b] = held("w3c", [P, N], U32, tag)
-            w3s[b] = held(f"w3s{b}", [P, N], U8)
-            nc.vector.quantize_mx(out=w3c[b][:].bitcast(FP8X4), scales=w3s[b][:], in_=w3g[b][:])
+        def w3_quant(b, reuses):
+            w3_w[b] = held("w3_w", [P, N], U32, reuses)
+            w3_s[b] = held(f"w3_s{b}", [P, N], U8)
+            nc.vector.quantize_mx(out=w3_w[b][:].bitcast(FP8X4), scales=w3_s[b][:], in_=w3_bf[b][:])
 
         def scores(pool, cols):
             width = cols.stop - cols.start
@@ -232,29 +238,29 @@ def tile_list_cast_review_scores_kernel(
                 acc = pool.tile([P, BANK], F32, name="acc")
                 for b in range(2):
                     nc.tensor.matmul_mx(
-                        out=acc[:, 0:width], lhsT=w3c[b][:, P * i : P * (i + 1)].bitcast(FP8X4),
-                        lhsT_scale=w3s[b][:, P * i : P * (i + 1)],
-                        rhs=yc[b][:, cols].bitcast(FP8X4), rhs_scale=ys[b][:, cols], start=(b == 0), stop=(b == 1),
+                        out=acc[:, 0:width], lhsT=w3_w[b][:, P * i : P * (i + 1)].bitcast(FP8X4),
+                        lhsT_scale=w3_s[b][:, P * i : P * (i + 1)],
+                        rhs=y_w[b][:, cols].bitcast(FP8X4), rhs_scale=y_s[b][:, cols],
+                        start=(b == 0), stop=(b == 1),
                     )
-                res = held(f"res{i}_{cols.start}", [P, width], F32)
-                nc.scalar.activation(out=res[:], in_=acc[:, 0:width], func=ACT.Tanh)
-                nc.sync.dma_start(out[P * i : P * (i + 1), cols], res[:])
+                result = held(f"result{i}_{cols.start}", [P, width], F32)
+                nc.scalar.activation(out=result[:], in_=acc[:, 0:width], func=ACT.Tanh)
+                nc.sync.dma_start(out[P * i : P * (i + 1), cols], result[:])
 
         for t in range(2):
             g_half(0, t, 0)
-        w1_round(0, 0, nc.vector.tensor_copy)
-        w1_quant(0, 0)
-        w1_round(1, 0, nc.vector.tensor_copy)
-        w1_quant(1, 0)
+        for a in range(2):
+            w1_round(a, 0, nc.vector.tensor_copy)
+            w1_quant(a, 0)
         for t in range(2):
             g_half(0, t, 1)
         for t in range(2, PACK):
             g_half(0, t, 0)
             g_half(0, t, 1)
-        w1_round(1, 1, nc.scalar.copy)
-        w1_round(0, 1, nc.scalar.copy)
-        w1_quant(1, 1)
-        w1_quant(0, 1)
+        for a in (1, 0):
+            w1_round(a, 1, nc.scalar.copy)
+        for a in (1, 0):
+            w1_quant(a, 1)
         for t in range(PACK):
             g_half(1, t, 0)
             g_half(1, t, 1)
@@ -268,16 +274,16 @@ def tile_list_cast_review_scores_kernel(
             look(1, t)
             pick(1, t)
             level(1, t)
-        w3_round(0)
-        w3_round(1)
-        halves = [slice(0, M // 2), slice(M // 2, M)]
+        w3_round(0, "h12")
+        w3_round(1, "h13")
+        runs = [slice(0, M // 2), slice(M // 2, M)]
         y_round(0, slice(0, M), "g13")
         w3_quant(0, "w1_high")
         y_quant(0, slice(0, M))
-        y_round(1, halves[0], "focus0")
+        y_round(1, runs[0], "focus0")
         w3_quant(1, "g13")
-        y_quant(1, halves[0])
-        y_round(1, halves[1], "focus0")
-        y_quant(1, halves[1])
-        scores(psum_g, halves[0])
-        scores(psum_h, halves[1])
+        y_quant(1, runs[0])
+        y_round(1, runs[1], "focus0")
+        y_quant(1, runs[1])
+        scores(psum_g, runs[0])
+        scores(psum_h, runs[1])

from contextlib import ExitStack

import concourse.mybir as mybir

K, T, S, M, H, N = 1024, 2048, 1024, 512, 1024, 384
FLOPS = 2 * (2 * K * H * S + H * N * M)

F32 = mybir.dt.float32
BF16 = mybir.dt.bfloat16
I32 = mybir.dt.int32
U32 = mybir.dt.uint32
U16 = mybir.dt.uint16
U8 = mybir.dt.uint8
FP8X4 = mybir.dt.float8_e4m3fn_x4
FP4X4 = mybir.dt.float4_e2m1fn_x4
ACT = mybir.ActivationFunctionType
ALU = mybir.AluOpType

P = 128
PACK = 4
KP = P * PACK
BANK = 512
GROUP = 16
QUADRANTS = 4
LAST_SCALE_ROW = 32 * (QUADRANTS - 1) + PACK
H_BANKS = 5
G_BANKS = 3


def tile_list_cast_review_scores_kernel(
    tc, tab_words, tab_scales, offs, pos1, pos2, w1, focus, w2_words, w2_scales,
    scale, stain, base, gain, w3, out,
):
    nc = tc.nc
    with ExitStack() as ctx:
        keep = ctx.enter_context(tc.tile_pool(name="keep", bufs=1))
        ring = ctx.enter_context(tc.tile_pool(name="ring", bufs=3))
        psum_h = ctx.enter_context(tc.psum_pool(name="psum_h", bufs=H_BANKS))
        psum_g = ctx.enter_context(tc.psum_pool(name="psum_g", bufs=G_BANKS))

        def held(name, shape, dtype, reuses=None):
            return keep.tile(shape, dtype, name=name, tag=reuses or name, align_bytes=64)

        offs_t = keep.tile([P, S // GROUP], U16, name="offs_t")
        pos1_t = keep.tile([P, M // GROUP], U16, name="pos1_t")
        pos2_t = keep.tile([P, M // GROUP], U16, name="pos2_t")

        tab_s = held("tab_s", [P, T], U8)
        w2_s_raw = held("w2_s_raw", [P, 2 * H], U8)
        v_s1 = held("v_s1", [P, S], U8)
        nc.gpsimd.memset(tab_s[:].bitcast(I32), 0)
        nc.vector.memset(w2_s_raw[:].bitcast(I32), 0)
        nc.vector.memset(v_s1[32 * (QUADRANTS - 1) :, :].bitcast(I32), 0)

        tab_w = [held(f"tab_w{a}", [P, T], U32) for a in range(2)]
        w2_w_raw = held("w2_w_raw", [P, 2, 2 * H], U8)
        w1_low = [held(f"w1_low{b}", [P, PACK, KP], F32) for b in range(2)]
        w1_high = held("w1_high", [P, PACK, H], F32)
        w1_raw = {
            (a, b): w1_high[:, :, b * KP : (b + 1) * KP] if a else w1_low[b][:] for a in range(2) for b in range(2)
        }
        focus_t = [held(f"focus{b}", [P, PACK, S], F32) for b in range(2)]
        w3_raw = [held(f"w3_raw{b}", [P, PACK, N], F32) for b in range(2)]

        def load_tab_words(a):
            nc.sync.dma_start(tab_w[a][:].bitcast(I32), tab_words[a].rearrange("p t i -> p (t i)").bitcast(I32))

        def load_row_values(name, vec):
            values = held(name, [P, 2, 2 * PACK], F32)
            nc.gpsimd.dma_start(values[:, :, 0:PACK], vec.rearrange("(b p t) -> p b t", b=2, t=PACK))
            return values

        def load_w1(dst, a, cols):
            nc.sync.dma_start(dst[:], w1[a * KP : (a + 1) * KP, cols].rearrange("(p j) c -> p j c", j=PACK))

        nc.sync.dma_start(offs_t[:], offs)
        for q in range(QUADRANTS):
            (nc.scalar if q < QUADRANTS // 2 else nc.sync).dma_start(
                tab_s[32 * q : 32 * q + 2 * PACK, :].bitcast(I32),
                tab_scales[:, PACK * q : PACK * (q + 1), :].bitcast(I32),
            )
        nc.sync.dma_start(pos2_t[:], pos2)
        load_tab_words(0)
        nc.sync.dma_start(w2_w_raw[:].bitcast(I32), w2_words.rearrange("a p c -> p a c").bitcast(I32))
        for q in range(QUADRANTS):
            nc.sync.dma_start(
                w2_s_raw[32 * q : 32 * q + PACK, :].bitcast(I32).rearrange("r (a c) -> r a c", a=2),
                w2_scales[:, PACK * q : PACK * (q + 1), :].bitcast(I32).rearrange("a r c -> r a c"),
            )
        load_tab_words(1)

        v_s0 = held("v_s0", [P, S], U8)
        nc.vector.tensor_copy(v_s0[:], tab_s[:].indirect(offs_t[:]))
        nc.sync.dma_start(v_s1[0:LAST_SCALE_ROW, :].bitcast(I32), v_s0[PACK : PACK + LAST_SCALE_ROW, :].bitcast(I32))
        v_s = [v_s0, v_s1]

        scale_t = load_row_values("scale_t", scale)
        stain_t = load_row_values("stain_t", stain)
        base_t = load_row_values("base_t", base)
        gain_t = load_row_values("gain_t", gain)
        load_w1(w1_low[0], 0, slice(0, KP))
        load_w1(w1_high, 1, slice(0, H))
        load_w1(w1_low[1], 0, slice(KP, H))
        nc.sync.dma_start(pos1_t[:], pos1)
        for b in range(2):
            rows = focus[b * KP : (b + 1) * KP, :].rearrange("(p t) s -> p t s", t=PACK)
            for t in range(PACK):
                nc.sync.dma_start(focus_t[b][:, t : t + 1, :], rows[:, t : t + 1, :])
        for b in range(2):
            nc.sync.dma_start(w3_raw[b][:], w3[b * KP : (b + 1) * KP, :].rearrange("(p j) n -> p j n", j=PACK))

        w2_w = [held(f"w2_w{b}", [P, 2, 2 * KP], U8) for b in range(2)]
        w2_s = [held(f"w2_s{b}", [P, 2, KP], U8) for b in range(2)]
        for b in range(2):
            nc.scalar.copy(
                w2_w[b][:].bitcast(U16).rearrange("p a (t m) -> p a t m", t=PACK),
                w2_w_raw[:].bitcast(U16)[:, :, b * KP : (b + 1) * KP].rearrange("p a (m t) -> p a t m", t=PACK),
            )
        v_w0 = held("v_w0", [P, S], U32)
        nc.vector.tensor_copy(v_w0[:], tab_w[0][:].indirect(offs_t[:]))
        for b in range(2):
            nc.vector.tensor_copy(
                w2_s[b][:].rearrange("p a (t m) -> p a t m", t=PACK),
                w2_s_raw[:].rearrange("p (a c) -> p a c", a=2)[:, :, b * KP : (b + 1) * KP].rearrange(
                    "p a (m t) -> p a t m", t=PACK
                ),
            )
        v_w = {}
        for half in range(S // BANK):
            v_w[0, half] = v_w0[:, half * BANK : (half + 1) * BANK]
            v_w1 = held(f"v_w1{half}", [P, BANK], U32)
            entries = offs_t[:, half * BANK // GROUP : (half + 1) * BANK // GROUP]
            nc.vector.tensor_copy(v_w1[:], tab_w[1][:].indirect(entries))
            v_w[1, half] = v_w1[:]

        def first_stage(pool, codes, scales, half):
            acc = pool.tile([P, BANK], F32, name="acc")
            for a in range(2):
                nc.tensor.matmul_mx(
                    out=acc[:], lhsT=codes[a], lhsT_scale=scales[a],
                    rhs=v_w[a, half].bitcast(FP8X4), rhs_scale=v_s[a][:, half * BANK : (half + 1) * BANK],
                    start=(a == 0), stop=(a == 1),
                )
            return acc

        picked = [w1_raw[0, 0], focus_t[1][:, :, 0:M]]
        levelled = [focus_t[0][:, :, 0:M], focus_t[1][:, :, 0:M]]
        looked = [w1_raw[1, 1], held("looked1", [P, PACK, M], F32)[:]]
        g = {(b, t): held(f"g{b}{t}", [P, S], F32) for b in range(2) for t in range(PACK)}
        h = {}

        def g_half(b, t, half):
            acc = first_stage(
                psum_g, [w2_w[b][:, a, 2 * P * t : 2 * P * (t + 1)].bitcast(FP4X4) for a in range(2)],
                [w2_s[b][:, a, P * t : P * (t + 1)] for a in range(2)], half,
            )
            nc.scalar.copy(g[b, t][:, half * BANK : (half + 1) * BANK], acc[:])

        def pick(b, t):
            nc.vector.tensor_copy(picked[b][:, t, :], g[b, t][:].indirect(pos2_t[:]))

        shift = held("shift", [P, 2, PACK], F32)
        nc.gpsimd.tensor_tensor(shift[:], base_t[:, :, 0:PACK], gain_t[:, :, 0:PACK], ALU.mult)
        nc.gpsimd.tensor_scalar(shift[:], shift[:], -1.0, 0.0, ALU.mult, ALU.add)

        def level(b, t):
            factor, offset = gain_t[:, b, t : t + 1], shift[:, b, t : t + 1]
            if (b, t) == (1, PACK - 1):
                nc.scalar.activation(
                    out=levelled[b][:, t, :], in_=picked[b][:, t, :], func=ACT.Identity, bias=offset, scale=factor
                )
            else:
                nc.gpsimd.tensor_scalar(levelled[b][:, t, :], picked[b][:, t, :], factor, offset, ALU.mult, ALU.add)

        w1_bf, w1_w, w1_s = {}, {}, {}

        def w1_round(a, b, copy):
            w1_bf[a, b] = ring.tile([P, PACK * KP], BF16, name="w1_bf", align_bytes=64)
            copy(
                w1_bf[a, b][:].rearrange("p (u e m j) -> p u m j e", u=2, e=2, j=PACK),
                w1_raw[a, b].rearrange("p j (m u e) -> p u m j e", u=2, e=2),
            )

        def w1_quant(a, b):
            w1_w[a, b] = held(f"w1_w{a}{b}", [P, KP], U32)
            w1_s[a, b] = held(f"w1_s{a}{b}", [P, KP], U8)
            nc.vector.quantize_mx(out=w1_w[a, b][:].bitcast(FP8X4), scales=w1_s[a, b][:], in_=w1_bf[a, b][:])

        def h_tile(b, t):
            h[b, t] = held(f"h{b}{t}", [P, S], F32)
            for half in range(S // BANK):
                cols = slice(half * BANK, (half + 1) * BANK)
                acc = first_stage(
                    psum_h, [w1_w[a, b][:, P * t : P * (t + 1)].bitcast(FP8X4) for a in range(2)],
                    [w1_s[a, b][:, P * t : P * (t + 1)] for a in range(2)], half,
                )
                nc.vector.tensor_tensor(h[b, t][:, cols], acc[:], focus_t[b][:, t, cols], ALU.add)

        def look(b, t):
            nc.scalar.activation(
                out=looked[b][:, t, :], in_=h[b, t][:].indirect(pos1_t[:]), func=ACT.Exp,
                bias=stain_t[:, b, t : t + 1], scale=scale_t[:, b, t : t + 1],
            )

        y_bf, w3_bf, w3_w, w3_s = {}, {}, {}, {}
        y_w = [held(f"y_w{b}", [P, M], U32) for b in range(2)]
        y_s = [held(f"y_s{b}", [P, M], U8) for b in range(2)]

        def y_round(b, cols, reuses):
            y_bf[b, cols.start] = held("y_bf", [P, PACK * (cols.stop - cols.start)], BF16, reuses)
            nc.vector.tensor_tensor(
                y_bf[b, cols.start][:].rearrange("p (c i t) -> p c t i", i=4, t=PACK),
                levelled[b][:, :, cols].rearrange("p t (c i) -> p c t i", i=4),
                looked[b][:, :, cols].rearrange("p t (c i) -> p c t i", i=4),
                ALU.mult,
            )

        def y_quant(b, cols):
            nc.vector.quantize_mx(
                out=y_w[b][:, cols].bitcast(FP8X4), scales=y_s[b][:, cols], in_=y_bf[b, cols.start][:]
            )

        def w3_round(b, reuses):
            w3_bf[b] = held("w3_bf", [P, PACK * N], BF16, reuses)
            nc.scalar.copy(
                w3_bf[b][:].rearrange("p (c i j) -> p c j i", i=4, j=PACK),
                w3_raw[b][:].rearrange("p j (c i) -> p c j i", i=4),
            )

        def w3_quant(b, reuses):
            w3_w[b] = held("w3_w", [P, N], U32, reuses)
            w3_s[b] = held(f"w3_s{b}", [P, N], U8)
            nc.vector.quantize_mx(out=w3_w[b][:].bitcast(FP8X4), scales=w3_s[b][:], in_=w3_bf[b][:])

        def scores(pool, cols):
            width = cols.stop - cols.start
            for i in range(N // P):
                acc = pool.tile([P, BANK], F32, name="acc")
                for b in range(2):
                    nc.tensor.matmul_mx(
                        out=acc[:, 0:width], lhsT=w3_w[b][:, P * i : P * (i + 1)].bitcast(FP8X4),
                        lhsT_scale=w3_s[b][:, P * i : P * (i + 1)],
                        rhs=y_w[b][:, cols].bitcast(FP8X4), rhs_scale=y_s[b][:, cols],
                        start=(b == 0), stop=(b == 1),
                    )
                result = held(f"result{i}_{cols.start}", [P, width], F32)
                nc.scalar.activation(out=result[:], in_=acc[:, 0:width], func=ACT.Tanh)
                nc.sync.dma_start(out[P * i : P * (i + 1), cols], result[:])

        for t in range(2):
            g_half(0, t, 0)
        for a in range(2):
            w1_round(a, 0, nc.vector.tensor_copy)
            w1_quant(a, 0)
        for t in range(2):
            g_half(0, t, 1)
        for t in range(2, PACK):
            g_half(0, t, 0)
            g_half(0, t, 1)
        for a in (1, 0):
            w1_round(a, 1, nc.scalar.copy)
        for a in (1, 0):
            w1_quant(a, 1)
        for t in range(PACK):
            g_half(1, t, 0)
            g_half(1, t, 1)
            h_tile(0, t)
            look(0, t)
        for t in range(PACK):
            pick(0, t)
            level(0, t)
        for t in range(PACK):
            h_tile(1, t)
            look(1, t)
            pick(1, t)
            level(1, t)
        w3_round(0, "h12")
        w3_round(1, "h13")
        runs = [slice(0, M // 2), slice(M // 2, M)]
        y_round(0, slice(0, M), "g13")
        w3_quant(0, "w1_high")
        y_quant(0, slice(0, M))
        y_round(1, runs[0], "focus0")
        w3_quant(1, "g13")
        y_quant(1, runs[0])
        y_round(1, runs[1], "focus0")
        y_quant(1, runs[1])
        scores(psum_g, runs[0])
        scores(psum_h, runs[1])
